import numpy as np
import ml_dtypes


def mxq(x, axis, fmt="e4m3"):
    dtype, down = {"e4m3": (ml_dtypes.float8_e4m3fn, 7), "e5m2": (ml_dtypes.float8_e5m2, 14)}[fmt]
    v = np.moveaxis(np.asarray(x, np.float32).astype(ml_dtypes.bfloat16).astype(np.float64), axis, -1)
    blocks = v.reshape(v.shape[:-1] + (-1, 32))
    amax = np.abs(blocks).max(-1, keepdims=True)
    byte = np.maximum(np.where(amax > 0, np.frexp(amax)[1] - 1 + 127, 0) - down, 1)
    scale = np.exp2(byte - 127.0)
    codes = (blocks / scale).astype(np.float32).astype(dtype).astype(np.float64)
    return np.moveaxis((codes * scale).reshape(v.shape), -1, axis)


WIDE = False


def mx_kscale(k):
    if not WIDE:
        return np.ones(k)
    levels = np.array([10, -10, 5, -5, 0])
    if k % 512:
        return np.exp2(np.random.permutation(np.resize(levels, k // 32))).repeat(32)
    a = np.empty((k // 512, 16))
    for p in range(k // 512):
        a[p, :8] = np.random.permutation(np.resize(levels, 8))
        for g in range(8):
            far = levels[np.abs(levels - a[p, g]) >= 10]
            a[p, g + 8] = far[np.random.randint(len(far))]
    return np.exp2(a.ravel()).repeat(32)


def f64(x):
    return np.asarray(x).astype(np.float64)


E2M1 = np.array([0.0, 0.5, 1.0, 1.5, 2.0, 3.0, 4.0, 6.0, -0.0, -0.5, -1.0, -1.5, -2.0, -3.0, -4.0, -6.0])


def pack_weight(w, fmt):
    k, n = w.shape
    w = f64(np.asarray(w, np.float32).astype(ml_dtypes.bfloat16)).reshape(k // 32, 32, n)
    amax = np.abs(w).max(1)
    if fmt == "e4m3":
        byte = np.frexp(amax)[1] - 1 + 127 - 7
    else:
        mant, ex = np.frexp(amax / 6.0)
        byte = np.where(mant > 0.5, ex, ex - 1) + 127
    byte = np.clip(np.where(amax > 0, byte, 1), 1, 254)
    scaled = (w * np.exp2(127.0 - byte)[:, None, :]).reshape(k, n).astype(np.float32)
    by_word = np.ascontiguousarray(scaled.reshape(k // 512, 128, 4, n).transpose(0, 1, 3, 2))
    if fmt == "e4m3":
        words = by_word.astype(ml_dtypes.float8_e4m3fn).view(np.uint8)
    else:
        c = by_word.astype(ml_dtypes.float4_e2m1fn).view(np.uint8) & 0xF
        words = (c[..., 0::2] | (c[..., 1::2] << 4)).reshape(k // 512, 128, 2 * n)
    return np.ascontiguousarray(words), np.ascontiguousarray(byte.astype(np.uint8).reshape(k // 512, 16, n))


def unpack_weight(words, scales, fmt):
    g, _, n = scales.shape
    words = np.ascontiguousarray(words).reshape(g, 128, n, -1)
    if fmt == "e4m3":
        vals = words.view(ml_dtypes.float8_e4m3fn).astype(np.float64)
    else:
        nib = np.empty((g, 128, n, 4), np.uint8)
        nib[..., 0::2] = words & 0xF
        nib[..., 1::2] = words >> 4
        vals = E2M1[nib]
    vals = vals * np.repeat(np.exp2(scales.astype(np.float64) - 127.0), 8, axis=1)[..., None]
    return vals.transpose(0, 1, 3, 2).reshape(g * 512, n)


K, L, T, N = 1024, 512, 512, 512


def setup_inputs():
    n = np.random.standard_normal
    fk = mx_kscale(K)
    fl = mx_kscale(L)
    xtp = pack_weight(n((K, T)) * np.random.uniform(0.3, 1.7, (1, T)) / fk[:, None], "e4m3")
    xsp = pack_weight(n((L, T)) / fl[:, None], "e2m1")
    wsp = pack_weight(n((L, N)) * 1 / np.sqrt(L) * fl[:, None], "e4m3")
    wcp = pack_weight(n((K, N)) * 1 / np.sqrt(K) * fk[:, None], "e2m1")
    return {
        "xt_words": xtp[0],
        "xt_scales": xtp[1],
        "wa": (n((K, N)) * 1 / np.sqrt(K) * fk[:, None]).astype(np.float32),
        "xs_words": xsp[0],
        "xs_scales": xsp[1],
        "ws_words": wsp[0],
        "ws_scales": wsp[1],
        "wc_words": wcp[0],
        "wc_scales": wcp[1],
    }


def reference(xt_words, xt_scales, wa, xs_words, xs_scales, ws_words, ws_scales, wc_words, wc_scales):
    xtu = unpack_weight(xt_words, xt_scales, "e4m3")
    xsu = unpack_weight(xs_words, xs_scales, "e2m1")
    wsu = unpack_weight(ws_words, ws_scales, "e4m3")
    wcu = unpack_weight(wc_words, wc_scales, "e2m1")
    waq = mxq(f64(wa), 0, "e4m3")
    a = xtu.T @ waq + xsu.T @ wsu
    b = xtu.T @ wcu
    sa = np.sqrt(np.mean(np.square(a), axis=1, keepdims=True) + 0.01)
    sb = np.sqrt(np.mean(np.square(b), axis=1, keepdims=True) + 0.01)
    y = a * sb / sa + 0.3 * b
    return y

from contextlib import ExitStack

import concourse.mybir as mybir

K, L, T, N = 1024, 512, 512, 512
FLOPS = 2 * T * N * (2 * K + L)

F32 = mybir.dt.float32
BF16 = mybir.dt.bfloat16
I32 = mybir.dt.int32
U32 = mybir.dt.uint32
U8 = mybir.dt.uint8
FP8X4 = mybir.dt.float8_e4m3fn_x4
FP4X4 = mybir.dt.float4_e2m1fn_x4
ACT = mybir.ActivationFunctionType
ALU = mybir.AluOpType

P = 128
TILES = T // P
HALF = N // 2
EPS = 0.01


def tile_mix_rows_sized_like_rival_kernel(
    tc, xt_words, xt_scales, wa, xs_words, xs_scales, ws_words, ws_scales, wc_words, wc_scales, out
):
    nc = tc.nc
    with ExitStack() as ctx:
        sb = ctx.enter_context(tc.tile_pool(name="sb", bufs=1))
        ps = ctx.enter_context(tc.psum_pool(name="ps", bufs=1))
        ctx.enter_context(tc.manual_schedule())

        xt_c = sb.tile([P, 2, T], U32, name="xt_c", align_bytes=64)
        ws_c = sb.tile([P, 1, N], U32, name="ws_c", align_bytes=64)
        wc_c = sb.tile([P, 2, 2 * N], U8, name="wc_c", align_bytes=64)
        xs_c = sb.tile([P, 1, 2 * T], U8, name="xs_c", align_bytes=64)
        xt_s = sb.tile([P, 2, T], U8, name="xt_s", align_bytes=64)
        wc_s = sb.tile([P, 2, N], U8, name="wc_s", align_bytes=64)
        xs_s = sb.tile([P, 1, T], U8, name="xs_s", align_bytes=64)
        ws_s = sb.tile([P, 1, N], U8, name="ws_s", align_bytes=64)
        wa_c = [sb.tile([P, N], U32, name="wa_c%d" % g, align_bytes=64) for g in range(2)]
        wa_s = [sb.tile([P, N], U8, name="wa_s%d" % g, align_bytes=64) for g in range(2)]
        raw = [sb.tile([P, 4, HALF], F32, name="raw%d" % i, align_bytes=64) for i in range(4)]
        grp = [sb.tile([P, HALF * 4], BF16, name="grp%d" % i, align_bytes=64) for i in range(4)]
        b_part = [sb.tile([P, N], F32, name="b_part%d" % i) for i in range(TILES)]
        res = [sb.tile([P, N], F32, name="res%d" % i) for i in range(TILES)]
        one = sb.tile([P, 1], F32, name="one")
        eps = sb.tile([P, 1], F32, name="eps")
        ssb = sb.tile([P, TILES], F32, name="ssb")
        inv_sb = sb.tile([P, TILES], F32, name="inv_sb")
        r_scale = sb.tile([P, TILES], F32, name="r_scale")
        r_bias = sb.tile([P, TILES], F32, name="r_bias")
        ssa = [sb.tile([P, 1], F32, name="ssa%d" % i) for i in range(TILES)]
        ratio = [sb.tile([P, 1], F32, name="ratio%d" % i) for i in range(TILES)]
        a_ps = [ps.tile([P, N], F32, name="a_ps%d" % i) for i in range(TILES)]
        b_ps = [ps.tile([P, N], F32, name="b_ps%d" % i) for i in range(TILES)]

        def load_scale_rows(eng, plane, scales, r):
            src = scales.bitcast(I32).rearrange("z (q r) c -> r q z c", r=4)[r]
            eng.dma_start(out=plane[r:P:32].bitcast(I32), in_=src)

        def load_e4m3(codes, words):
            nc.sync.dma_start(out=codes[:].bitcast(I32), in_=words.rearrange("z p n t -> p z (n t)").bitcast(I32))

        def load_e2m1(codes, words):
            nc.sync.dma_start(out=codes[:].bitcast(I32), in_=words.rearrange("z p n -> p z n").bitcast(I32))

        def load_wa(i):
            g, h = divmod(i, 2)
            src = wa[512 * g : 512 * (g + 1), HALF * h : HALF * (h + 1)].rearrange("(p j) w -> p j w", j=4)
            nc.sync.dma_start(out=raw[i][:], in_=src)

        def cast(i, c0, c1):
            nc.vector.tensor_copy(
                out=grp[i][:, 4 * c0 : 4 * c1].rearrange("p (c i t) -> p c t i", i=4, t=4),
                in_=raw[i][:, :, c0:c1].rearrange("p t (c i) -> p c t i", i=4),
            )

        def quant(i, c0, c1):
            g, h = divmod(i, 2)
            cols = slice(HALF * h + c0, HALF * h + c1)
            nc.vector.quantize_mx(
                out=wa_c[g][:, cols].bitcast(FP8X4), scales=wa_s[g][:, cols], in_=grp[i][:, 4 * c0 : 4 * c1]
            )

        def tok(i):
            return slice(P * i, P * (i + 1))

        def mm_b(i, g):
            nc.tensor.matmul_mx(
                out=b_ps[i][:],
                lhsT=xt_c[:, g, tok(i)].bitcast(FP8X4),
                lhsT_scale=xt_s[:, g, tok(i)],
                rhs=wc_c[:, g, :].bitcast(FP4X4),
                rhs_scale=wc_s[:, g, :],
                start=(g == 0),
                stop=(g == 1),
            )

        def mm_wa(i, g, cols, start=False, stop=False):
            nc.tensor.matmul_mx(
                out=a_ps[i][:, cols],
                lhsT=xt_c[:, g, tok(i)].bitcast(FP8X4),
                lhsT_scale=xt_s[:, g, tok(i)],
                rhs=wa_c[g][:, cols].bitcast(FP8X4),
                rhs_scale=wa_s[g][:, cols],
                start=start,
                stop=stop,
            )

        def mm_ws(i, stop=False):
            nc.tensor.matmul_mx(
                out=a_ps[i][:],
                lhsT=xs_c[:, 0, 2 * P * i : 2 * P * (i + 1)].bitcast(FP4X4),
                lhsT_scale=xs_s[:, 0, tok(i)],
                rhs=ws_c[:, 0, :].bitcast(FP8X4),
                rhs_scale=ws_s[:, 0, :],
                start=False,
                stop=stop,
            )

        nc.vector.memset(xt_s[:].bitcast(I32), 0)
        nc.vector.memset(wc_s[:].bitcast(I32), 0)
        nc.vector.memset(one[:], 1.0)
        nc.vector.memset(xs_s[:].bitcast(I32), 0)
        nc.gpsimd.memset(ws_s[:].bitcast(I32), 0)
        nc.scalar.activation(out=eps[:], in_=one[:], func=ACT.Abs_reciprocal_sqrt, scale=1.0 / (EPS * EPS))
        for r in range(4):
            load_scale_rows(nc.gpsimd, ws_s, ws_scales, r)

        load_e4m3(xt_c, xt_words)
        for r in range(4):
            load_scale_rows(nc.sync, xt_s, xt_scales, r)
        load_e2m1(wc_c, wc_words)
        load_wa(0)
        for r in range(4):
            load_scale_rows(nc.sync, wc_s, wc_scales, r)
        load_wa(1)
        load_wa(2)
        load_wa(3)
        for r in range(4):
            load_scale_rows(nc.sync, xs_s, xs_scales, r)
        load_e2m1(xs_c, xs_words)
        load_e4m3(ws_c, ws_words)

        for i in range(TILES):
            mm_b(i, 0)
            mm_b(i, 1)
        for i in range(TILES):
            nc.scalar.activation(out=b_part[i][:], in_=b_ps[i][:], func=ACT.Square, accum_out=ssb[:, i : i + 1])
        nc.scalar.activation(out=inv_sb[:], in_=ssb[:], func=ACT.Abs_reciprocal_sqrt, scale=1.0 / N, bias=eps[:])
        nc.scalar.activation(out=b_part[0][:], in_=b_ps[0][:], func=ACT.Copy, scale=0.3)
        nc.scalar.activation(out=r_scale[:], in_=inv_sb[:], func=ACT.Square, scale=N**-0.5)
        nc.scalar.activation(out=r_bias[:], in_=inv_sb[:], func=ACT.Square, scale=EPS**0.5)
        nc.scalar.activation(out=b_part[1][:], in_=b_ps[1][:], func=ACT.Copy, scale=0.3)

        cast(0, 0, HALF)
        cast(1, 0, HALF)
        quant(0, 0, HALF)
        cast(2, 0, HALF)
        quant(1, 0, HALF)
        quant(2, 0, HALF)
        cast(3, 0, 128)
        cast(3, 128, 256)
        quant(3, 0, 128)
        quant(3, 128, 256)
        for i in (2, 3):
            nc.vector.tensor_scalar(out=b_part[i][:], in0=b_ps[i][:], scalar1=0.3, scalar2=None, op0=ALU.mult)

        every, low, high = slice(0, N), slice(0, HALF), slice(HALF, N)
        for i in (0, 1, 2):
            mm_wa(i, 0, every, start=True)
        mm_wa(0, 1, low)
        mm_wa(1, 1, low)
        for i in (0, 1):
            mm_ws(i)
            mm_wa(i, 1, high, stop=True)
        mm_wa(2, 1, every)
        mm_ws(2, stop=True)
        mm_wa(3, 0, every, start=True)
        mm_wa(3, 1, every)
        mm_ws(3, stop=True)

        for i in range(TILES):
            nc.scalar.activation(out=res[i][:], in_=a_ps[i][:], func=ACT.Square, accum_out=ssa[i][:])
            nc.scalar.activation(
                out=ratio[i][:],
                in_=ssa[i][:],
                func=ACT.Abs_reciprocal_sqrt,
                scale=r_scale[:, i : i + 1],
                bias=r_bias[:, i : i + 1],
            )
            nc.vector.scalar_tensor_tensor(
                out=res[i][:], in0=a_ps[i][:], scalar=ratio[i][:], in1=b_part[i][:], op0=ALU.mult, op1=ALU.add
            )
            nc.sync.dma_start(out=out[tok(i), :], in_=res[i][:])
